import numpy as np
import ml_dtypes


def mxq(x, axis, fmt="e4m3"):
    dtype, down = {"e4m3": (ml_dtypes.float8_e4m3fn, 7), "e5m2": (ml_dtypes.float8_e5m2, 14)}[fmt]
    v = np.moveaxis(np.asarray(x, np.float32).astype(ml_dtypes.bfloat16).astype(np.float64), axis, -1)
    blocks = v.reshape(v.shape[:-1] + (-1, 32))
    amax = np.abs(blocks).max(-1, keepdims=True)
    byte = np.maximum(np.where(amax > 0, np.frexp(amax)[1] - 1 + 127, 0) - down, 1)
    scale = np.exp2(byte - 127.0)
    codes = (blocks / scale).astype(np.float32).astype(dtype).astype(np.float64)
    return np.moveaxis((codes * scale).reshape(v.shape), -1, axis)


WIDE = False


def mx_kscale(k):
    if not WIDE:
        return np.ones(k)
    levels = np.array([10, -10, 5, -5, 0])
    if k % 512:
        return np.exp2(np.random.permutation(np.resize(levels, k // 32))).repeat(32)
    a = np.empty((k // 512, 16))
    for p in range(k // 512):
        a[p, :8] = np.random.permutation(np.resize(levels, 8))
        for g in range(8):
            far = levels[np.abs(levels - a[p, g]) >= 10]
            a[p, g + 8] = far[np.random.randint(len(far))]
    return np.exp2(a.ravel()).repeat(32)


def f64(x):
    return np.asarray(x).astype(np.float64)


def striped(idx):
    return np.tile(idx.reshape(-1, 16).T, (8, 1)).astype(np.uint16)


def unstriped(offs):
    return offs[:16].T.reshape(-1).astype(np.int64)


def pack_weight(w):
    k, n = w.shape
    w = f64(np.asarray(w, np.float32).astype(ml_dtypes.bfloat16)).reshape(k // 32, 32, n)
    amax = np.abs(w).max(1)
    byte = np.clip(np.where(amax > 0, np.frexp(amax)[1] - 1 + 127 - 7, 1), 1, 254)
    scaled = (w * np.exp2(127.0 - byte)[:, None, :]).reshape(k, n).astype(np.float32)
    words = np.ascontiguousarray(scaled.reshape(k // 512, 128, 4, n).transpose(0, 1, 3, 2)).astype(ml_dtypes.float8_e4m3fn).view(np.uint8)
    return words, np.ascontiguousarray(byte.astype(np.uint8).reshape(k // 512, 16, n))


def unpack_weight(words, scales):
    g, p, n, _ = words.shape
    vals = np.ascontiguousarray(words).view(ml_dtypes.float8_e4m3fn).astype(np.float64) * np.repeat(np.exp2(scales.astype(np.float64) - 127.0), 8, axis=1)[..., None]
    return vals.transpose(0, 1, 3, 2).reshape(g * 512, n)


def sigmoid(v):
    return 1.0 / (1.0 + np.exp(-np.maximum(v, -700.0)))


K, T, S, V, N, D = 512, 1024, 512, 256, 128, 3
P = 2 ** 7


def setup_inputs():
    n = np.random.standard_normal
    s = mx_kscale(K)[:, None]
    packed_xT = pack_weight(n((K, T)) * s)
    return {
        "x_words": packed_xT[0],
        "x_scales": packed_xT[1],
        "w1": (n((K, N)) / np.sqrt(K) / s).astype(np.float32),
        "iou": (np.tile(np.random.uniform(0.0, 0.9, (D, 1, V)), (1, P, 1))).astype(np.float32),
        "offs": striped(np.random.permutation(T)[:S]),
        "cen": striped(np.random.permutation(S)[:V]),
        "pos1": striped(np.random.permutation(S)[:V]),
        "pos2": striped(np.random.permutation(S)[:V]),
        "pos3": striped(np.random.permutation(S)[:V]),
    }


def reference(x_words, x_scales, w1, iou, offs, cen, pos1, pos2, pos3):
    xq = unpack_weight(x_words, x_scales)[:, unstriped(offs)]
    p = sigmoid(mxq(f64(w1), 0, "e4m3").T @ xq)
    pc = p[:, unstriped(cen)]
    s0 = -1.0 * (p[:, unstriped(pos1)] * f64(iou)[0, :1]) + 1.0
    s1 = -1.0 * (p[:, unstriped(pos2)] * f64(iou)[1, :1]) + 1.0
    s2 = -1.0 * (p[:, unstriped(pos3)] * f64(iou)[2, :1]) + 1.0
    return pc * ((s0 * s1) * s2)

@@ -1,0 +1,98 @@
+from contextlib import ExitStack
+
+import concourse.mybir as mybir
+
+F32 = mybir.dt.float32
+BF16 = mybir.dt.bfloat16
+I32 = mybir.dt.int32
+U32 = mybir.dt.uint32
+U16 = mybir.dt.uint16
+U8 = mybir.dt.uint8
+FP8X4 = mybir.dt.float8_e4m3fn_x4
+ALU = mybir.AluOpType
+ACT = mybir.ActivationFunctionType
+
+P = 128
+K, T, S, V, M, D = 512, 1024, 512, 256, 128, 3
+PIECES = (256, 128, 128)
+FLOPS = 2 * K * M * S
+
+
+def tile_picked_ynms_lin_p_kernel(tc, x_words, x_scales, w1, iou, offs, cen, pos1, pos2, pos3, out):
+    nc = tc.nc
+    with ExitStack() as ctx:
+        sb = ctx.enter_context(tc.tile_pool(name="sb", bufs=1))
+        ps = ctx.enter_context(tc.psum_pool(name="ps", bufs=1))
+
+        offs_sb = sb.tile([P, S // 16], U16, name="offs_sb")
+        cen_sb = sb.tile([P, V // 16], U16, name="cen_sb")
+        pos1_sb = sb.tile([P, V // 16], U16, name="pos1_sb")
+        pos2_sb = sb.tile([P, V // 16], U16, name="pos2_sb")
+        pos3_sb = sb.tile([P, V // 16], U16, name="pos3_sb")
+        words = sb.tile([P, T], U32, name="words", align_bytes=64)
+        scales = sb.tile([P, T], U8, name="scales", align_bytes=64)
+        w_raw = sb.tile([P, 4, M], F32, name="w_raw", align_bytes=64)
+        iou_sb = sb.tile([P, D, V], F32, name="iou_sb", align_bytes=64)
+
+        nc.vector.memset(scales[:].bitcast(I32), 0)
+        warm_in = sb.tile([P, 1], F32, name="warm_in")
+        warm_out = sb.tile([P, 1], F32, name="warm_out")
+        nc.vector.memset(warm_in[:], 0.0)
+
+        nc.sync.dma_start(offs_sb[:], offs)
+        nc.sync.dma_start(w_raw[:], w1.rearrange("(p j) m -> p j m", j=4))
+        nc.sync.dma_start(pos1_sb[:], pos1)
+        nc.sync.dma_start(words[:].bitcast(I32), x_words[0].rearrange("p n t -> p (n t)").bitcast(I32))
+        for q in range(4):
+            nc.scalar.dma_start(scales[32 * q : 32 * q + 4, :].bitcast(I32), x_scales[0, 4 * q : 4 * q + 4, :].bitcast(I32))
+        nc.scalar.activation(warm_out[:], warm_in[:], ACT.Sigmoid)
+        nc.sync.dma_start(iou_sb[:], iou.rearrange("d p v -> p d v"))
+        nc.sync.dma_start(cen_sb[:], cen)
+        nc.sync.dma_start(pos2_sb[:], pos2)
+        nc.sync.dma_start(pos3_sb[:], pos3)
+
+        w_bf = sb.tile([P, M, 4], BF16, name="w_bf", align_bytes=64)
+        nc.scalar.copy(w_bf[:], w_raw[:].rearrange("p j m -> p m j"))
+
+        picked_scales = sb.tile([P, S], U8, name="picked_scales", align_bytes=64)
+        nc.vector.tensor_copy(picked_scales[:], scales[:].indirect(offs_sb[:]))
+
+        w_codes = sb.tile([P, M], U32, name="w_codes", align_bytes=64)
+        w_scales = sb.tile([P, M], U8, name="w_scales", align_bytes=64)
+        nc.vector.quantize_mx(w_codes[:].bitcast(FP8X4), w_scales[:], w_bf[:].rearrange("p m j -> p (m j)"))
+
+        prob = sb.tile([P, S], F32, name="prob", align_bytes=64)
+        logit = sb.tile([P, S], F32, name="logit", align_bytes=64)
+        banks = []
+        c0 = 0
+        for i, n in enumerate(PIECES):
+            picked = sb.tile([P, n], U32, name="picked%d" % i, align_bytes=64)
+            nc.vector.tensor_copy(picked[:], words[:].indirect(offs_sb[:, c0 // 16 : (c0 + n) // 16]))
+            bank = ps.tile([P, n], F32, name="bank%d" % i)
+            nc.tensor.matmul_mx(bank[:], lhsT=w_codes[:].bitcast(FP8X4), lhsT_scale=w_scales[:], rhs=picked[:].bitcast(FP8X4), rhs_scale=picked_scales[:, c0 : c0 + n], start=True, stop=True)
+            nc.scalar.activation(prob[:, c0 : c0 + n], bank[:], ACT.Sigmoid)
+            banks.append((bank, c0, n))
+            c0 = c0 + n
+        for bank, b0, n in banks[:-1]:
+            nc.vector.tensor_copy(logit[:, b0 : b0 + n], bank[:])
+        bank, b0, n = banks[-1]
+        nc.scalar.copy(logit[:, b0 : b0 + n], bank[:])
+
+        pc = sb.tile([P, V], F32, name="pc")
+        g2 = sb.tile([P, V], F32, name="g2")
+        nc.scalar.activation(pc[:], logit[:].indirect(cen_sb[:]), ACT.Sigmoid)
+        nc.scalar.activation(g2[:], logit[:].indirect(pos3_sb[:]), ACT.Sigmoid)
+
+        t0 = sb.tile([P, V], F32, name="t0")
+        t1 = sb.tile([P, V], F32, name="t1")
+        t2 = sb.tile([P, V], F32, name="t2")
+        u = sb.tile([P, V], F32, name="u")
+        w = sb.tile([P, V], F32, name="w")
+        res = sb.tile([P, V], F32, name="res")
+        nc.vector.tensor_tensor(t0[:], prob[:].indirect(pos1_sb[:]), iou_sb[:, 0, :], ALU.mult)
+        nc.vector.tensor_tensor(t1[:], prob[:].indirect(pos2_sb[:]), iou_sb[:, 1, :], ALU.mult)
+        nc.vector.scalar_tensor_tensor(u[:], t0[:], 1.0, pc[:], ALU.subtract, ALU.mult)
+        nc.vector.scalar_tensor_tensor(t2[:], g2[:], -1.0, iou_sb[:, 2, :], ALU.mult, ALU.mult)
+        nc.vector.scalar_tensor_tensor(w[:], t1[:], 1.0, u[:], ALU.subtract, ALU.mult)
+        nc.vector.scalar_tensor_tensor(res[:], t2[:], 1.0, w[:], ALU.add, ALU.mult)
+        nc.sync.dma_start(out, res[:])

@@ -14,7 +14,7 @@ ACT = mybir.ActivationFunctionType
 
 P = 128
 K, T, S, V, M, D = 512, 1024, 512, 256, 128, 3
-PIECES = (256, 128, 128)
+PIECES = (128, 128, 128, 128)
 FLOPS = 2 * K * M * S
 
 
@@ -40,16 +40,17 @@ def tile_picked_ynms_lin_p_kernel(tc, x_words, x_scales, w1, iou, offs, cen, pos
         nc.vector.memset(warm_in[:], 0.0)
 
         nc.sync.dma_start(offs_sb[:], offs)
-        nc.sync.dma_start(w_raw[:], w1.rearrange("(p j) m -> p j m", j=4))
-        nc.sync.dma_start(pos1_sb[:], pos1)
-        nc.sync.dma_start(words[:].bitcast(I32), x_words[0].rearrange("p n t -> p (n t)").bitcast(I32))
+        nc.scalar.dma_start(w_raw[:], w1.rearrange("(p j) m -> p j m", j=4))
         for q in range(4):
-            nc.scalar.dma_start(scales[32 * q : 32 * q + 4, :].bitcast(I32), x_scales[0, 4 * q : 4 * q + 4, :].bitcast(I32))
+            queue = nc.sync if q < 2 else nc.scalar
+            queue.dma_start(scales[32 * q : 32 * q + 4, :].bitcast(I32), x_scales[0, 4 * q : 4 * q + 4, :].bitcast(I32))
+        nc.sync.dma_start(words[:].bitcast(I32), x_words[0].rearrange("p n t -> p (n t)").bitcast(I32))
         nc.scalar.activation(warm_out[:], warm_in[:], ACT.Sigmoid)
-        nc.sync.dma_start(iou_sb[:], iou.rearrange("d p v -> p d v"))
-        nc.sync.dma_start(cen_sb[:], cen)
+        nc.sync.dma_start(pos1_sb[:], pos1)
         nc.sync.dma_start(pos2_sb[:], pos2)
+        nc.sync.dma_start(cen_sb[:], cen)
         nc.sync.dma_start(pos3_sb[:], pos3)
+        nc.sync.dma_start(iou_sb[:], iou.rearrange("d p v -> p d v"))
 
         w_bf = sb.tile([P, M, 4], BF16, name="w_bf", align_bytes=64)
         nc.scalar.copy(w_bf[:], w_raw[:].rearrange("p j m -> p m j"))
@@ -93,6 +94,9 @@ def tile_picked_ynms_lin_p_kernel(tc, x_words, x_scales, w1, iou, offs, cen, pos
         nc.vector.tensor_tensor(t1[:], prob[:].indirect(pos2_sb[:]), iou_sb[:, 1, :], ALU.mult)
         nc.vector.scalar_tensor_tensor(u[:], t0[:], 1.0, pc[:], ALU.subtract, ALU.mult)
         nc.vector.scalar_tensor_tensor(t2[:], g2[:], -1.0, iou_sb[:, 2, :], ALU.mult, ALU.mult)
-        nc.vector.scalar_tensor_tensor(w[:], t1[:], 1.0, u[:], ALU.subtract, ALU.mult)
-        nc.vector.scalar_tensor_tensor(res[:], t2[:], 1.0, w[:], ALU.add, ALU.mult)
-        nc.sync.dma_start(out, res[:])
+        halves = (slice(0, V // 2), slice(V // 2, V))
+        for h in halves:
+            nc.vector.scalar_tensor_tensor(w[:, h], t1[:, h], 1.0, u[:, h], ALU.subtract, ALU.mult)
+        for h in halves:
+            nc.vector.scalar_tensor_tensor(res[:, h], t2[:, h], 1.0, w[:, h], ALU.add, ALU.mult)
+            nc.sync.dma_start(out[:, h], res[:, h])

@@ -82,7 +82,9 @@ def tile_picked_ynms_lin_p_kernel(tc, x_words, x_scales, w1, iou, offs, cen, pos
         pc = sb.tile([P, V], F32, name="pc")
         g2 = sb.tile([P, V], F32, name="g2")
         nc.scalar.activation(pc[:], logit[:].indirect(cen_sb[:]), ACT.Sigmoid)
-        nc.scalar.activation(g2[:], logit[:].indirect(pos3_sb[:]), ACT.Sigmoid)
+        halves = (slice(0, V // 2), slice(V // 2, V))
+        for h in halves:
+            nc.scalar.activation(g2[:, h], logit[:].indirect(pos3_sb[:, h.start // 16 : h.stop // 16]), ACT.Sigmoid)
 
         t0 = sb.tile([P, V], F32, name="t0")
         t1 = sb.tile([P, V], F32, name="t1")
@@ -93,9 +95,8 @@ def tile_picked_ynms_lin_p_kernel(tc, x_words, x_scales, w1, iou, offs, cen, pos
         nc.vector.tensor_tensor(t0[:], prob[:].indirect(pos1_sb[:]), iou_sb[:, 0, :], ALU.mult)
         nc.vector.tensor_tensor(t1[:], prob[:].indirect(pos2_sb[:]), iou_sb[:, 1, :], ALU.mult)
         nc.vector.scalar_tensor_tensor(u[:], t0[:], 1.0, pc[:], ALU.subtract, ALU.mult)
-        nc.vector.scalar_tensor_tensor(t2[:], g2[:], -1.0, iou_sb[:, 2, :], ALU.mult, ALU.mult)
-        halves = (slice(0, V // 2), slice(V // 2, V))
         for h in halves:
+            nc.vector.scalar_tensor_tensor(t2[:, h], g2[:, h], -1.0, iou_sb[:, 2, h], ALU.mult, ALU.mult)
             nc.vector.scalar_tensor_tensor(w[:, h], t1[:, h], 1.0, u[:, h], ALU.subtract, ALU.mult)
         for h in halves:
             nc.vector.scalar_tensor_tensor(res[:, h], t2[:, h], 1.0, w[:, h], ALU.add, ALU.mult)

@@ -46,11 +46,11 @@ def tile_picked_ynms_lin_p_kernel(tc, x_words, x_scales, w1, iou, offs, cen, pos
             queue.dma_start(scales[32 * q : 32 * q + 4, :].bitcast(I32), x_scales[0, 4 * q : 4 * q + 4, :].bitcast(I32))
         nc.sync.dma_start(words[:].bitcast(I32), x_words[0].rearrange("p n t -> p (n t)").bitcast(I32))
         nc.scalar.activation(warm_out[:], warm_in[:], ACT.Sigmoid)
+        nc.sync.dma_start(iou_sb[:], iou.rearrange("d p v -> p d v"))
         nc.sync.dma_start(pos1_sb[:], pos1)
         nc.sync.dma_start(pos2_sb[:], pos2)
         nc.sync.dma_start(cen_sb[:], cen)
         nc.sync.dma_start(pos3_sb[:], pos3)
-        nc.sync.dma_start(iou_sb[:], iou.rearrange("d p v -> p d v"))
 
         w_bf = sb.tile([P, M, 4], BF16, name="w_bf", align_bytes=64)
         nc.scalar.copy(w_bf[:], w_raw[:].rearrange("p j m -> p m j"))
@@ -94,10 +94,12 @@ def tile_picked_ynms_lin_p_kernel(tc, x_words, x_scales, w1, iou, offs, cen, pos
         res = sb.tile([P, V], F32, name="res")
         nc.vector.tensor_tensor(t0[:], prob[:].indirect(pos1_sb[:]), iou_sb[:, 0, :], ALU.mult)
         nc.vector.tensor_tensor(t1[:], prob[:].indirect(pos2_sb[:]), iou_sb[:, 1, :], ALU.mult)
-        nc.vector.scalar_tensor_tensor(u[:], t0[:], 1.0, pc[:], ALU.subtract, ALU.mult)
+        for h in halves:
+            nc.vector.scalar_tensor_tensor(u[:, h], t0[:, h], 1.0, pc[:, h], ALU.subtract, ALU.mult)
+        for h in halves:
+            nc.vector.scalar_tensor_tensor(w[:, h], t1[:, h], 1.0, u[:, h], ALU.subtract, ALU.mult)
         for h in halves:
             nc.vector.scalar_tensor_tensor(t2[:, h], g2[:, h], -1.0, iou_sb[:, 2, h], ALU.mult, ALU.mult)
-            nc.vector.scalar_tensor_tensor(w[:, h], t1[:, h], 1.0, u[:, h], ALU.subtract, ALU.mult)
         for h in halves:
             nc.vector.scalar_tensor_tensor(res[:, h], t2[:, h], 1.0, w[:, h], ALU.add, ALU.mult)
             nc.sync.dma_start(out[:, h], res[:, h])

@@ -31,7 +31,9 @@ def tile_picked_ynms_lin_p_kernel(tc, x_words, x_scales, w1, iou, offs, cen, pos
         pos3_sb = sb.tile([P, V // 16], U16, name="pos3_sb")
         words = sb.tile([P, T], U32, name="words", align_bytes=64)
         scales = sb.tile([P, T], U8, name="scales", align_bytes=64)
-        w_raw = sb.tile([P, 4, M], F32, name="w_raw", align_bytes=64)
+        w_lo = sb.tile([P, 2, M], F32, name="w_lo", align_bytes=64)
+        w_hi = sb.tile([P, 2, M], F32, name="w_hi", tag="late", align_bytes=64)
+        w_rows = w1.rearrange("(p j) m -> p j m", j=4)
         iou_sb = sb.tile([P, D, V], F32, name="iou_sb", align_bytes=64)
 
         nc.vector.memset(scales[:].bitcast(I32), 0)
@@ -40,11 +42,12 @@ def tile_picked_ynms_lin_p_kernel(tc, x_words, x_scales, w1, iou, offs, cen, pos
         nc.vector.memset(warm_in[:], 0.0)
 
         nc.sync.dma_start(offs_sb[:], offs)
-        nc.scalar.dma_start(w_raw[:], w1.rearrange("(p j) m -> p j m", j=4))
+        nc.scalar.dma_start(w_lo[:], w_rows[:, 0:2, :])
         for q in range(4):
             queue = nc.sync if q < 2 else nc.scalar
             queue.dma_start(scales[32 * q : 32 * q + 4, :].bitcast(I32), x_scales[0, 4 * q : 4 * q + 4, :].bitcast(I32))
         nc.sync.dma_start(words[:].bitcast(I32), x_words[0].rearrange("p n t -> p (n t)").bitcast(I32))
+        nc.sync.dma_start(w_hi[:], w_rows[:, 2:4, :])
         nc.scalar.activation(warm_out[:], warm_in[:], ACT.Sigmoid)
         nc.sync.dma_start(iou_sb[:], iou.rearrange("d p v -> p d v"))
         nc.sync.dma_start(pos1_sb[:], pos1)
@@ -53,7 +56,8 @@ def tile_picked_ynms_lin_p_kernel(tc, x_words, x_scales, w1, iou, offs, cen, pos
         nc.sync.dma_start(pos3_sb[:], pos3)
 
         w_bf = sb.tile([P, M, 4], BF16, name="w_bf", align_bytes=64)
-        nc.scalar.copy(w_bf[:], w_raw[:].rearrange("p j m -> p m j"))
+        nc.scalar.copy(w_bf[:, :, 0:2], w_lo[:].rearrange("p j m -> p m j"))
+        nc.scalar.copy(w_bf[:, :, 2:4], w_hi[:].rearrange("p j m -> p m j"))
 
         picked_scales = sb.tile([P, S], U8, name="picked_scales", align_bytes=64)
         nc.vector.tensor_copy(picked_scales[:], scales[:].indirect(offs_sb[:]))
@@ -67,7 +71,7 @@ def tile_picked_ynms_lin_p_kernel(tc, x_words, x_scales, w1, iou, offs, cen, pos
         banks = []
         c0 = 0
         for i, n in enumerate(PIECES):
-            picked = sb.tile([P, n], U32, name="picked%d" % i, align_bytes=64)
+            picked = sb.tile([P, n], U32, name="picked%d" % i, tag="late" if i == len(PIECES) - 1 else "picked%d" % i, align_bytes=64)
             nc.vector.tensor_copy(picked[:], words[:].indirect(offs_sb[:, c0 // 16 : (c0 + n) // 16]))
             bank = ps.tile([P, n], F32, name="bank%d" % i)
             nc.tensor.matmul_mx(bank[:], lhsT=w_codes[:].bitcast(FP8X4), lhsT_scale=w_scales[:], rhs=picked[:].bitcast(FP8X4), rhs_scale=picked_scales[:, c0 : c0 + n], start=True, stop=True)

@@ -32,23 +32,19 @@ def tile_picked_ynms_lin_p_kernel(tc, x_words, x_scales, w1, iou, offs, cen, pos
         words = sb.tile([P, T], U32, name="words", align_bytes=64)
         scales = sb.tile([P, T], U8, name="scales", align_bytes=64)
         w_lo = sb.tile([P, 2, M], F32, name="w_lo", align_bytes=64)
-        w_hi = sb.tile([P, 2, M], F32, name="w_hi", tag="late", align_bytes=64)
+        w_hi = sb.tile([P, 2, M], F32, name="w_hi", align_bytes=64)
         w_rows = w1.rearrange("(p j) m -> p j m", j=4)
         iou_sb = sb.tile([P, D, V], F32, name="iou_sb", align_bytes=64)
 
         nc.vector.memset(scales[:].bitcast(I32), 0)
-        warm_in = sb.tile([P, 1], F32, name="warm_in")
-        warm_out = sb.tile([P, 1], F32, name="warm_out")
-        nc.vector.memset(warm_in[:], 0.0)
 
         nc.sync.dma_start(offs_sb[:], offs)
         nc.scalar.dma_start(w_lo[:], w_rows[:, 0:2, :])
         for q in range(4):
             queue = nc.sync if q < 2 else nc.scalar
             queue.dma_start(scales[32 * q : 32 * q + 4, :].bitcast(I32), x_scales[0, 4 * q : 4 * q + 4, :].bitcast(I32))
-        nc.sync.dma_start(words[:].bitcast(I32), x_words[0].rearrange("p n t -> p (n t)").bitcast(I32))
         nc.sync.dma_start(w_hi[:], w_rows[:, 2:4, :])
-        nc.scalar.activation(warm_out[:], warm_in[:], ACT.Sigmoid)
+        nc.sync.dma_start(words[:].bitcast(I32), x_words[0].rearrange("p n t -> p (n t)").bitcast(I32))
         nc.sync.dma_start(iou_sb[:], iou.rearrange("d p v -> p d v"))
         nc.sync.dma_start(pos1_sb[:], pos1)
         nc.sync.dma_start(pos2_sb[:], pos2)
@@ -70,11 +66,12 @@ def tile_picked_ynms_lin_p_kernel(tc, x_words, x_scales, w1, iou, offs, cen, pos
         logit = sb.tile([P, S], F32, name="logit", align_bytes=64)
         banks = []
         c0 = 0
+        picked_words = sb.tile([P, S], U32, name="picked_words", align_bytes=64)
         for i, n in enumerate(PIECES):
-            picked = sb.tile([P, n], U32, name="picked%d" % i, tag="late" if i == len(PIECES) - 1 else "picked%d" % i, align_bytes=64)
-            nc.vector.tensor_copy(picked[:], words[:].indirect(offs_sb[:, c0 // 16 : (c0 + n) // 16]))
+            picked = picked_words[:, c0 : c0 + n]
+            nc.vector.tensor_copy(picked, words[:].indirect(offs_sb[:, c0 // 16 : (c0 + n) // 16]))
             bank = ps.tile([P, n], F32, name="bank%d" % i)
-            nc.tensor.matmul_mx(bank[:], lhsT=w_codes[:].bitcast(FP8X4), lhsT_scale=w_scales[:], rhs=picked[:].bitcast(FP8X4), rhs_scale=picked_scales[:, c0 : c0 + n], start=True, stop=True)
+            nc.tensor.matmul_mx(bank[:], lhsT=w_codes[:].bitcast(FP8X4), lhsT_scale=w_scales[:], rhs=picked.bitcast(FP8X4), rhs_scale=picked_scales[:, c0 : c0 + n], start=True, stop=True)
             nc.scalar.activation(prob[:, c0 : c0 + n], bank[:], ACT.Sigmoid)
             banks.append((bank, c0, n))
             c0 = c0 + n

@@ -31,19 +31,19 @@ def tile_picked_ynms_lin_p_kernel(tc, x_words, x_scales, w1, iou, offs, cen, pos
         pos3_sb = sb.tile([P, V // 16], U16, name="pos3_sb")
         words = sb.tile([P, T], U32, name="words", align_bytes=64)
         scales = sb.tile([P, T], U8, name="scales", align_bytes=64)
-        w_lo = sb.tile([P, 2, M], F32, name="w_lo", align_bytes=64)
-        w_hi = sb.tile([P, 2, M], F32, name="w_hi", align_bytes=64)
+        w_lo = sb.tile([P, 3, M], F32, name="w_lo", align_bytes=64)
+        w_hi = sb.tile([P, 1, M], F32, name="w_hi", align_bytes=64)
         w_rows = w1.rearrange("(p j) m -> p j m", j=4)
         iou_sb = sb.tile([P, D, V], F32, name="iou_sb", align_bytes=64)
 
         nc.vector.memset(scales[:].bitcast(I32), 0)
 
         nc.sync.dma_start(offs_sb[:], offs)
-        nc.scalar.dma_start(w_lo[:], w_rows[:, 0:2, :])
+        nc.scalar.dma_start(w_lo[:], w_rows[:, 0:3, :])
         for q in range(4):
             queue = nc.sync if q < 2 else nc.scalar
             queue.dma_start(scales[32 * q : 32 * q + 4, :].bitcast(I32), x_scales[0, 4 * q : 4 * q + 4, :].bitcast(I32))
-        nc.sync.dma_start(w_hi[:], w_rows[:, 2:4, :])
+        nc.sync.dma_start(w_hi[:], w_rows[:, 3:4, :])
         nc.sync.dma_start(words[:].bitcast(I32), x_words[0].rearrange("p n t -> p (n t)").bitcast(I32))
         nc.sync.dma_start(iou_sb[:], iou.rearrange("d p v -> p d v"))
         nc.sync.dma_start(pos1_sb[:], pos1)
@@ -52,8 +52,8 @@ def tile_picked_ynms_lin_p_kernel(tc, x_words, x_scales, w1, iou, offs, cen, pos
         nc.sync.dma_start(pos3_sb[:], pos3)
 
         w_bf = sb.tile([P, M, 4], BF16, name="w_bf", align_bytes=64)
-        nc.scalar.copy(w_bf[:, :, 0:2], w_lo[:].rearrange("p j m -> p m j"))
-        nc.scalar.copy(w_bf[:, :, 2:4], w_hi[:].rearrange("p j m -> p m j"))
+        nc.scalar.copy(w_bf[:, :, 0:3], w_lo[:].rearrange("p j m -> p m j"))
+        nc.scalar.copy(w_bf[:, :, 3:4], w_hi[:].rearrange("p j m -> p m j"))
 
         picked_scales = sb.tile([P, S], U8, name="picked_scales", align_bytes=64)
         nc.vector.tensor_copy(picked_scales[:], scales[:].indirect(offs_sb[:]))

@@ -38,11 +38,11 @@ def tile_picked_ynms_lin_p_kernel(tc, x_words, x_scales, w1, iou, offs, cen, pos
 
         nc.vector.memset(scales[:].bitcast(I32), 0)
 
-        nc.sync.dma_start(offs_sb[:], offs)
-        nc.scalar.dma_start(w_lo[:], w_rows[:, 0:3, :])
+        nc.sync.dma_start(w_lo[:], w_rows[:, 0:3, :])
         for q in range(4):
             queue = nc.sync if q < 2 else nc.scalar
             queue.dma_start(scales[32 * q : 32 * q + 4, :].bitcast(I32), x_scales[0, 4 * q : 4 * q + 4, :].bitcast(I32))
+        nc.sync.dma_start(offs_sb[:], offs)
         nc.sync.dma_start(w_hi[:], w_rows[:, 3:4, :])
         nc.sync.dma_start(words[:].bitcast(I32), x_words[0].rearrange("p n t -> p (n t)").bitcast(I32))
         nc.sync.dma_start(iou_sb[:], iou.rearrange("d p v -> p d v"))

@@ -31,19 +31,18 @@ def tile_picked_ynms_lin_p_kernel(tc, x_words, x_scales, w1, iou, offs, cen, pos
         pos3_sb = sb.tile([P, V // 16], U16, name="pos3_sb")
         words = sb.tile([P, T], U32, name="words", align_bytes=64)
         scales = sb.tile([P, T], U8, name="scales", align_bytes=64)
-        w_lo = sb.tile([P, 3, M], F32, name="w_lo", align_bytes=64)
-        w_hi = sb.tile([P, 1, M], F32, name="w_hi", align_bytes=64)
+        w_raw = sb.tile([P, 4, M], F32, name="w_raw", align_bytes=64)
         w_rows = w1.rearrange("(p j) m -> p j m", j=4)
         iou_sb = sb.tile([P, D, V], F32, name="iou_sb", align_bytes=64)
 
         nc.vector.memset(scales[:].bitcast(I32), 0)
 
-        nc.sync.dma_start(w_lo[:], w_rows[:, 0:3, :])
+        nc.sync.dma_start(w_raw[:, 0:3, :], w_rows[:, 0:3, :])
         for q in range(4):
             queue = nc.sync if q < 2 else nc.scalar
             queue.dma_start(scales[32 * q : 32 * q + 4, :].bitcast(I32), x_scales[0, 4 * q : 4 * q + 4, :].bitcast(I32))
         nc.sync.dma_start(offs_sb[:], offs)
-        nc.sync.dma_start(w_hi[:], w_rows[:, 3:4, :])
+        nc.sync.dma_start(w_raw[:, 3:4, :], w_rows[:, 3:4, :])
         nc.sync.dma_start(words[:].bitcast(I32), x_words[0].rearrange("p n t -> p (n t)").bitcast(I32))
         nc.sync.dma_start(iou_sb[:], iou.rearrange("d p v -> p d v"))
         nc.sync.dma_start(pos1_sb[:], pos1)
@@ -51,9 +50,13 @@ def tile_picked_ynms_lin_p_kernel(tc, x_words, x_scales, w1, iou, offs, cen, pos
         nc.sync.dma_start(cen_sb[:], cen)
         nc.sync.dma_start(pos3_sb[:], pos3)
 
+        warm_in = sb.tile([P, 8], F32, name="warm_in")
+        warm_out = sb.tile([P, 8], F32, name="warm_out")
+        nc.vector.memset(warm_in[:], 0.0)
+        nc.scalar.activation(warm_out[:, 0:1], warm_in[:, 0:1], ACT.Sigmoid)
         w_bf = sb.tile([P, M, 4], BF16, name="w_bf", align_bytes=64)
-        nc.scalar.copy(w_bf[:, :, 0:3], w_lo[:].rearrange("p j m -> p m j"))
-        nc.scalar.copy(w_bf[:, :, 3:4], w_hi[:].rearrange("p j m -> p m j"))
+        nc.vector.tensor_copy(w_bf[:, :, 0:2], w_raw[:, 0:2, :].rearrange("p j m -> p m j"))
+        nc.scalar.copy(w_bf[:, :, 2:4], w_raw[:, 2:4, :].rearrange("p j m -> p m j"))
 
         picked_scales = sb.tile([P, S], U8, name="picked_scales", align_bytes=64)
         nc.vector.tensor_copy(picked_scales[:], scales[:].indirect(offs_sb[:]))

@@ -50,12 +50,9 @@ def tile_picked_ynms_lin_p_kernel(tc, x_words, x_scales, w1, iou, offs, cen, pos
         nc.sync.dma_start(cen_sb[:], cen)
         nc.sync.dma_start(pos3_sb[:], pos3)
 
-        warm_in = sb.tile([P, 8], F32, name="warm_in")
-        warm_out = sb.tile([P, 8], F32, name="warm_out")
-        nc.vector.memset(warm_in[:], 0.0)
-        nc.scalar.activation(warm_out[:, 0:1], warm_in[:, 0:1], ACT.Sigmoid)
         w_bf = sb.tile([P, M, 4], BF16, name="w_bf", align_bytes=64)
-        nc.vector.tensor_copy(w_bf[:, :, 0:2], w_raw[:, 0:2, :].rearrange("p j m -> p m j"))
+        nc.scalar.copy(w_bf[:, 0:8, 0:2], w_raw[:, 0:2, 0:8].rearrange("p j m -> p m j"))
+        nc.vector.tensor_copy(w_bf[:, 8:M, 0:2], w_raw[:, 0:2, 8:M].rearrange("p j m -> p m j"))
         nc.scalar.copy(w_bf[:, :, 2:4], w_raw[:, 2:4, :].rearrange("p j m -> p m j"))
 
         picked_scales = sb.tile([P, S], U8, name="picked_scales", align_bytes=64)

@@ -37,12 +37,12 @@ def tile_picked_ynms_lin_p_kernel(tc, x_words, x_scales, w1, iou, offs, cen, pos
 
         nc.vector.memset(scales[:].bitcast(I32), 0)
 
-        nc.sync.dma_start(w_raw[:, 0:3, :], w_rows[:, 0:3, :])
-        for q in range(4):
-            queue = nc.sync if q < 2 else nc.scalar
-            queue.dma_start(scales[32 * q : 32 * q + 4, :].bitcast(I32), x_scales[0, 4 * q : 4 * q + 4, :].bitcast(I32))
         nc.sync.dma_start(offs_sb[:], offs)
-        nc.sync.dma_start(w_raw[:, 3:4, :], w_rows[:, 3:4, :])
+        nc.scalar.dma_start(w_raw[:, 0:3, :], w_rows[:, 0:3, :])
+        for q in range(4):
+            queue = nc.sync if q < 3 else nc.scalar
+            queue.dma_start(scales[32 * q : 32 * q + 4, :].bitcast(I32), x_scales[0, 4 * q : 4 * q + 4, :].bitcast(I32))
+        nc.scalar.dma_start(w_raw[:, 3:4, :], w_rows[:, 3:4, :])
         nc.sync.dma_start(words[:].bitcast(I32), x_words[0].rearrange("p n t -> p (n t)").bitcast(I32))
         nc.sync.dma_start(iou_sb[:], iou.rearrange("d p v -> p d v"))
         nc.sync.dma_start(pos1_sb[:], pos1)

@@ -37,12 +37,12 @@ def tile_picked_ynms_lin_p_kernel(tc, x_words, x_scales, w1, iou, offs, cen, pos
 
         nc.vector.memset(scales[:].bitcast(I32), 0)
 
+        nc.sync.dma_start(w_raw[:, 0:3, :], w_rows[:, 0:3, :])
         nc.sync.dma_start(offs_sb[:], offs)
-        nc.scalar.dma_start(w_raw[:, 0:3, :], w_rows[:, 0:3, :])
         for q in range(4):
             queue = nc.sync if q < 3 else nc.scalar
             queue.dma_start(scales[32 * q : 32 * q + 4, :].bitcast(I32), x_scales[0, 4 * q : 4 * q + 4, :].bitcast(I32))
-        nc.scalar.dma_start(w_raw[:, 3:4, :], w_rows[:, 3:4, :])
+        nc.sync.dma_start(w_raw[:, 3:4, :], w_rows[:, 3:4, :])
         nc.sync.dma_start(words[:].bitcast(I32), x_words[0].rearrange("p n t -> p (n t)").bitcast(I32))
         nc.sync.dma_start(iou_sb[:], iou.rearrange("d p v -> p d v"))
         nc.sync.dma_start(pos1_sb[:], pos1)

@@ -14,8 +14,8 @@ ACT = mybir.ActivationFunctionType
 
 P = 128
 K, T, S, V, M, D = 512, 1024, 512, 256, 128, 3
-PIECES = (128, 128, 128, 128)
 FLOPS = 2 * K * M * S
+PIECES = (128, 128, 128, 64, 64)
 
 
 def tile_picked_ynms_lin_p_kernel(tc, x_words, x_scales, w1, iou, offs, cen, pos1, pos2, pos3, out):
@@ -44,11 +44,11 @@ def tile_picked_ynms_lin_p_kernel(tc, x_words, x_scales, w1, iou, offs, cen, pos
             queue.dma_start(scales[32 * q : 32 * q + 4, :].bitcast(I32), x_scales[0, 4 * q : 4 * q + 4, :].bitcast(I32))
         nc.sync.dma_start(w_raw[:, 3:4, :], w_rows[:, 3:4, :])
         nc.sync.dma_start(words[:].bitcast(I32), x_words[0].rearrange("p n t -> p (n t)").bitcast(I32))
-        nc.sync.dma_start(iou_sb[:], iou.rearrange("d p v -> p d v"))
+        nc.sync.dma_start(pos3_sb[:], pos3)
+        nc.sync.dma_start(cen_sb[:], cen)
         nc.sync.dma_start(pos1_sb[:], pos1)
         nc.sync.dma_start(pos2_sb[:], pos2)
-        nc.sync.dma_start(cen_sb[:], cen)
-        nc.sync.dma_start(pos3_sb[:], pos3)
+        nc.sync.dma_start(iou_sb[:], iou.rearrange("d p v -> p d v"))
 
         w_bf = sb.tile([P, M, 4], BF16, name="w_bf", align_bytes=64)
         nc.scalar.copy(w_bf[:, 0:8, 0:2], w_raw[:, 0:2, 0:8].rearrange("p j m -> p m j"))
@@ -63,44 +63,47 @@ def tile_picked_ynms_lin_p_kernel(tc, x_words, x_scales, w1, iou, offs, cen, pos
         nc.vector.quantize_mx(w_codes[:].bitcast(FP8X4), w_scales[:], w_bf[:].rearrange("p m j -> p (m j)"))
 
         prob = sb.tile([P, S], F32, name="prob", align_bytes=64)
-        logit = sb.tile([P, S], F32, name="logit", align_bytes=64)
-        banks = []
-        c0 = 0
         picked_words = sb.tile([P, S], U32, name="picked_words", align_bytes=64)
+        c0 = 0
         for i, n in enumerate(PIECES):
             picked = picked_words[:, c0 : c0 + n]
             nc.vector.tensor_copy(picked, words[:].indirect(offs_sb[:, c0 // 16 : (c0 + n) // 16]))
             bank = ps.tile([P, n], F32, name="bank%d" % i)
             nc.tensor.matmul_mx(bank[:], lhsT=w_codes[:].bitcast(FP8X4), lhsT_scale=w_scales[:], rhs=picked.bitcast(FP8X4), rhs_scale=picked_scales[:, c0 : c0 + n], start=True, stop=True)
             nc.scalar.activation(prob[:, c0 : c0 + n], bank[:], ACT.Sigmoid)
-            banks.append((bank, c0, n))
             c0 = c0 + n
-        for bank, b0, n in banks[:-1]:
-            nc.vector.tensor_copy(logit[:, b0 : b0 + n], bank[:])
-        bank, b0, n = banks[-1]
-        nc.scalar.copy(logit[:, b0 : b0 + n], bank[:])
+
+        a, b = slice(0, V // 2), slice(V // 2, V)
+
+        def entries(tile, h):
+            return tile[:, h.start // 16 : h.stop // 16]
 
         pc = sb.tile([P, V], F32, name="pc")
+        g1 = sb.tile([P, V // 2], F32, name="g1")
         g2 = sb.tile([P, V], F32, name="g2")
-        nc.scalar.activation(pc[:], logit[:].indirect(cen_sb[:]), ACT.Sigmoid)
-        halves = (slice(0, V // 2), slice(V // 2, V))
-        for h in halves:
-            nc.scalar.activation(g2[:, h], logit[:].indirect(pos3_sb[:, h.start // 16 : h.stop // 16]), ACT.Sigmoid)
+        nc.scalar.activation(g2[:, b], prob[:].indirect(entries(pos3_sb, b)), ACT.Copy)
+        nc.scalar.activation(pc[:, a], prob[:].indirect(entries(cen_sb, a)), ACT.Copy)
+        nc.scalar.activation(pc[:, b], prob[:].indirect(entries(cen_sb, b)), ACT.Copy)
+        nc.scalar.activation(g2[:, a], prob[:].indirect(entries(pos3_sb, a)), ACT.Copy)
+        nc.scalar.activation(g1[:], prob[:].indirect(entries(pos2_sb, b)), ACT.Copy)
 
         t0 = sb.tile([P, V], F32, name="t0")
-        t1 = sb.tile([P, V], F32, name="t1")
-        t2 = sb.tile([P, V], F32, name="t2")
+        t1a = sb.tile([P, V // 2], F32, name="t1a")
+        t2b = sb.tile([P, V // 2], F32, name="t2b")
         u = sb.tile([P, V], F32, name="u")
         w = sb.tile([P, V], F32, name="w")
         res = sb.tile([P, V], F32, name="res")
         nc.vector.tensor_tensor(t0[:], prob[:].indirect(pos1_sb[:]), iou_sb[:, 0, :], ALU.mult)
-        nc.vector.tensor_tensor(t1[:], prob[:].indirect(pos2_sb[:]), iou_sb[:, 1, :], ALU.mult)
-        for h in halves:
+        nc.vector.tensor_tensor(t1a[:], prob[:].indirect(entries(pos2_sb, a)), iou_sb[:, 1, a], ALU.mult)
+        nc.vector.scalar_tensor_tensor(t2b[:], g2[:, b], -1.0, iou_sb[:, 2, b], ALU.mult, ALU.mult)
+        for h in (a, b):
             nc.vector.scalar_tensor_tensor(u[:, h], t0[:, h], 1.0, pc[:, h], ALU.subtract, ALU.mult)
-        for h in halves:
-            nc.vector.scalar_tensor_tensor(w[:, h], t1[:, h], 1.0, u[:, h], ALU.subtract, ALU.mult)
-        for h in halves:
-            nc.vector.scalar_tensor_tensor(t2[:, h], g2[:, h], -1.0, iou_sb[:, 2, h], ALU.mult, ALU.mult)
-        for h in halves:
-            nc.vector.scalar_tensor_tensor(res[:, h], t2[:, h], 1.0, w[:, h], ALU.add, ALU.mult)
-            nc.sync.dma_start(out[:, h], res[:, h])
+        nc.vector.scalar_tensor_tensor(w[:, a], t1a[:], 1.0, u[:, a], ALU.subtract, ALU.mult)
+        nc.vector.scalar_tensor_tensor(w[:, b], t2b[:], 1.0, u[:, b], ALU.add, ALU.mult)
+        last = u
+        nc.vector.scalar_tensor_tensor(last[:, a], g2[:, a], -1.0, iou_sb[:, 2, a], ALU.mult, ALU.mult)
+        nc.vector.tensor_tensor(last[:, b], g1[:], iou_sb[:, 1, b], ALU.mult)
+        nc.vector.scalar_tensor_tensor(res[:, a], last[:, a], 1.0, w[:, a], ALU.add, ALU.mult)
+        nc.sync.dma_start(out[:, a], res[:, a])
+        nc.vector.scalar_tensor_tensor(res[:, b], last[:, b], 1.0, w[:, b], ALU.subtract, ALU.mult)
+        nc.sync.dma_start(out[:, b], res[:, b])

@@ -15,7 +15,8 @@ ACT = mybir.ActivationFunctionType
 P = 128
 K, T, S, V, M, D = 512, 1024, 512, 256, 128, 3
 FLOPS = 2 * K * M * S
-PIECES = (128, 128, 128, 64, 64)
+GATHERS = (256, 128, 64, 64)
+PRODUCTS = (128, 128, 128, 64, 64)
 
 
 def tile_picked_ynms_lin_p_kernel(tc, x_words, x_scales, w1, iou, offs, cen, pos1, pos2, pos3, out):
@@ -44,11 +45,11 @@ def tile_picked_ynms_lin_p_kernel(tc, x_words, x_scales, w1, iou, offs, cen, pos
             queue.dma_start(scales[32 * q : 32 * q + 4, :].bitcast(I32), x_scales[0, 4 * q : 4 * q + 4, :].bitcast(I32))
         nc.sync.dma_start(w_raw[:, 3:4, :], w_rows[:, 3:4, :])
         nc.sync.dma_start(words[:].bitcast(I32), x_words[0].rearrange("p n t -> p (n t)").bitcast(I32))
-        nc.sync.dma_start(pos3_sb[:], pos3)
-        nc.sync.dma_start(cen_sb[:], cen)
+        nc.sync.dma_start(iou_sb[:], iou.rearrange("d p v -> p d v"))
         nc.sync.dma_start(pos1_sb[:], pos1)
         nc.sync.dma_start(pos2_sb[:], pos2)
-        nc.sync.dma_start(iou_sb[:], iou.rearrange("d p v -> p d v"))
+        nc.sync.dma_start(cen_sb[:], cen)
+        nc.sync.dma_start(pos3_sb[:], pos3)
 
         w_bf = sb.tile([P, M, 4], BF16, name="w_bf", align_bytes=64)
         nc.scalar.copy(w_bf[:, 0:8, 0:2], w_raw[:, 0:2, 0:8].rearrange("p j m -> p m j"))
@@ -65,45 +66,39 @@ def tile_picked_ynms_lin_p_kernel(tc, x_words, x_scales, w1, iou, offs, cen, pos
         prob = sb.tile([P, S], F32, name="prob", align_bytes=64)
         picked_words = sb.tile([P, S], U32, name="picked_words", align_bytes=64)
         c0 = 0
-        for i, n in enumerate(PIECES):
-            picked = picked_words[:, c0 : c0 + n]
-            nc.vector.tensor_copy(picked, words[:].indirect(offs_sb[:, c0 // 16 : (c0 + n) // 16]))
+        for n in GATHERS:
+            nc.vector.tensor_copy(picked_words[:, c0 : c0 + n], words[:].indirect(offs_sb[:, c0 // 16 : (c0 + n) // 16]))
+            c0 = c0 + n
+        c0 = 0
+        for i, n in enumerate(PRODUCTS):
+            cols = slice(c0, c0 + n)
             bank = ps.tile([P, n], F32, name="bank%d" % i)
-            nc.tensor.matmul_mx(bank[:], lhsT=w_codes[:].bitcast(FP8X4), lhsT_scale=w_scales[:], rhs=picked.bitcast(FP8X4), rhs_scale=picked_scales[:, c0 : c0 + n], start=True, stop=True)
-            nc.scalar.activation(prob[:, c0 : c0 + n], bank[:], ACT.Sigmoid)
+            nc.tensor.matmul_mx(bank[:], lhsT=w_codes[:].bitcast(FP8X4), lhsT_scale=w_scales[:], rhs=picked_words[:, cols].bitcast(FP8X4), rhs_scale=picked_scales[:, cols], start=True, stop=True)
+            nc.scalar.activation(prob[:, cols], bank[:], ACT.Sigmoid)
             c0 = c0 + n
 
-        a, b = slice(0, V // 2), slice(V // 2, V)
-
-        def entries(tile, h):
-            return tile[:, h.start // 16 : h.stop // 16]
+        halves = (slice(0, V // 2), slice(V // 2, V))
 
         pc = sb.tile([P, V], F32, name="pc")
-        g1 = sb.tile([P, V // 2], F32, name="g1")
         g2 = sb.tile([P, V], F32, name="g2")
-        nc.scalar.activation(g2[:, b], prob[:].indirect(entries(pos3_sb, b)), ACT.Copy)
-        nc.scalar.activation(pc[:, a], prob[:].indirect(entries(cen_sb, a)), ACT.Copy)
-        nc.scalar.activation(pc[:, b], prob[:].indirect(entries(cen_sb, b)), ACT.Copy)
-        nc.scalar.activation(g2[:, a], prob[:].indirect(entries(pos3_sb, a)), ACT.Copy)
-        nc.scalar.activation(g1[:], prob[:].indirect(entries(pos2_sb, b)), ACT.Copy)
+        nc.scalar.activation(pc[:], prob[:].indirect(cen_sb[:]), ACT.Copy)
+        for h in halves:
+            nc.scalar.activation(g2[:, h], prob[:].indirect(pos3_sb[:, h.start // 16 : h.stop // 16]), ACT.Copy)
 
         t0 = sb.tile([P, V], F32, name="t0")
-        t1a = sb.tile([P, V // 2], F32, name="t1a")
-        t2b = sb.tile([P, V // 2], F32, name="t2b")
+        t1 = sb.tile([P, V], F32, name="t1")
         u = sb.tile([P, V], F32, name="u")
         w = sb.tile([P, V], F32, name="w")
         res = sb.tile([P, V], F32, name="res")
         nc.vector.tensor_tensor(t0[:], prob[:].indirect(pos1_sb[:]), iou_sb[:, 0, :], ALU.mult)
-        nc.vector.tensor_tensor(t1a[:], prob[:].indirect(entries(pos2_sb, a)), iou_sb[:, 1, a], ALU.mult)
-        nc.vector.scalar_tensor_tensor(t2b[:], g2[:, b], -1.0, iou_sb[:, 2, b], ALU.mult, ALU.mult)
-        for h in (a, b):
+        nc.vector.tensor_tensor(t1[:], prob[:].indirect(pos2_sb[:]), iou_sb[:, 1, :], ALU.mult)
+        for h in halves:
             nc.vector.scalar_tensor_tensor(u[:, h], t0[:, h], 1.0, pc[:, h], ALU.subtract, ALU.mult)
-        nc.vector.scalar_tensor_tensor(w[:, a], t1a[:], 1.0, u[:, a], ALU.subtract, ALU.mult)
-        nc.vector.scalar_tensor_tensor(w[:, b], t2b[:], 1.0, u[:, b], ALU.add, ALU.mult)
-        last = u
-        nc.vector.scalar_tensor_tensor(last[:, a], g2[:, a], -1.0, iou_sb[:, 2, a], ALU.mult, ALU.mult)
-        nc.vector.tensor_tensor(last[:, b], g1[:], iou_sb[:, 1, b], ALU.mult)
-        nc.vector.scalar_tensor_tensor(res[:, a], last[:, a], 1.0, w[:, a], ALU.add, ALU.mult)
-        nc.sync.dma_start(out[:, a], res[:, a])
-        nc.vector.scalar_tensor_tensor(res[:, b], last[:, b], 1.0, w[:, b], ALU.subtract, ALU.mult)
-        nc.sync.dma_start(out[:, b], res[:, b])
+        for h in halves:
+            nc.vector.scalar_tensor_tensor(w[:, h], t1[:, h], 1.0, u[:, h], ALU.subtract, ALU.mult)
+        t2 = sb.tile([P, V], F32, name="t2")
+        for h in halves:
+            nc.vector.scalar_tensor_tensor(t2[:, h], g2[:, h], -1.0, iou_sb[:, 2, h], ALU.mult, ALU.mult)
+        for h in halves:
+            nc.vector.scalar_tensor_tensor(res[:, h], t2[:, h], 1.0, w[:, h], ALU.add, ALU.mult)
+            nc.sync.dma_start(out[:, h], res[:, h])

@@ -77,28 +77,35 @@ def tile_picked_ynms_lin_p_kernel(tc, x_words, x_scales, w1, iou, offs, cen, pos
             nc.scalar.activation(prob[:, cols], bank[:], ACT.Sigmoid)
             c0 = c0 + n
 
-        halves = (slice(0, V // 2), slice(V // 2, V))
+        h, q = slice(0, 128), slice(128, V)
+        q2, q3 = slice(128, 192), slice(192, V)
+
+        def entries(tile, cols):
+            return tile[:, cols.start // 16 : cols.stop // 16]
 
         pc = sb.tile([P, V], F32, name="pc")
         g2 = sb.tile([P, V], F32, name="g2")
         nc.scalar.activation(pc[:], prob[:].indirect(cen_sb[:]), ACT.Copy)
-        for h in halves:
-            nc.scalar.activation(g2[:, h], prob[:].indirect(pos3_sb[:, h.start // 16 : h.stop // 16]), ACT.Copy)
+        for cols in (h, q):
+            nc.scalar.activation(g2[:, cols], prob[:].indirect(entries(pos3_sb, cols)), ACT.Copy)
 
         t0 = sb.tile([P, V], F32, name="t0")
         t1 = sb.tile([P, V], F32, name="t1")
+        t2 = sb.tile([P, V], F32, name="t2")
         u = sb.tile([P, V], F32, name="u")
         w = sb.tile([P, V], F32, name="w")
         res = sb.tile([P, V], F32, name="res")
         nc.vector.tensor_tensor(t0[:], prob[:].indirect(pos1_sb[:]), iou_sb[:, 0, :], ALU.mult)
         nc.vector.tensor_tensor(t1[:], prob[:].indirect(pos2_sb[:]), iou_sb[:, 1, :], ALU.mult)
-        for h in halves:
-            nc.vector.scalar_tensor_tensor(u[:, h], t0[:, h], 1.0, pc[:, h], ALU.subtract, ALU.mult)
-        for h in halves:
-            nc.vector.scalar_tensor_tensor(w[:, h], t1[:, h], 1.0, u[:, h], ALU.subtract, ALU.mult)
-        t2 = sb.tile([P, V], F32, name="t2")
-        for h in halves:
-            nc.vector.scalar_tensor_tensor(t2[:, h], g2[:, h], -1.0, iou_sb[:, 2, h], ALU.mult, ALU.mult)
-        for h in halves:
-            nc.vector.scalar_tensor_tensor(res[:, h], t2[:, h], 1.0, w[:, h], ALU.add, ALU.mult)
-            nc.sync.dma_start(out[:, h], res[:, h])
+        for cols in (h, q):
+            nc.vector.scalar_tensor_tensor(u[:, cols], t0[:, cols], 1.0, pc[:, cols], ALU.subtract, ALU.mult)
+        nc.vector.scalar_tensor_tensor(t2[:, h], g2[:, h], -1.0, iou_sb[:, 2, h], ALU.mult, ALU.mult)
+        nc.vector.scalar_tensor_tensor(w[:, h], t1[:, h], 1.0, u[:, h], ALU.subtract, ALU.mult)
+        nc.vector.scalar_tensor_tensor(t2[:, q], g2[:, q], -1.0, iou_sb[:, 2, q], ALU.mult, ALU.mult)
+        for cols in (q2, q3):
+            nc.vector.scalar_tensor_tensor(w[:, cols], t1[:, cols], 1.0, u[:, cols], ALU.subtract, ALU.mult)
+        nc.vector.scalar_tensor_tensor(res[:, h], t2[:, h], 1.0, w[:, h], ALU.add, ALU.mult)
+        nc.sync.dma_start(out[:, h], res[:, h])
+        for cols in (q2, q3):
+            nc.vector.scalar_tensor_tensor(res[:, cols], t2[:, cols], 1.0, w[:, cols], ALU.add, ALU.mult)
+        nc.sync.dma_start(out[:, q], res[:, q])

@@ -38,12 +38,11 @@ def tile_picked_ynms_lin_p_kernel(tc, x_words, x_scales, w1, iou, offs, cen, pos
 
         nc.vector.memset(scales[:].bitcast(I32), 0)
 
-        nc.sync.dma_start(w_raw[:, 0:3, :], w_rows[:, 0:3, :])
+        nc.sync.dma_start(w_raw[:], w_rows)
         nc.sync.dma_start(offs_sb[:], offs)
         for q in range(4):
             queue = nc.sync if q < 3 else nc.scalar
             queue.dma_start(scales[32 * q : 32 * q + 4, :].bitcast(I32), x_scales[0, 4 * q : 4 * q + 4, :].bitcast(I32))
-        nc.sync.dma_start(w_raw[:, 3:4, :], w_rows[:, 3:4, :])
         nc.sync.dma_start(words[:].bitcast(I32), x_words[0].rearrange("p n t -> p (n t)").bitcast(I32))
         nc.sync.dma_start(iou_sb[:], iou.rearrange("d p v -> p d v"))
         nc.sync.dma_start(pos1_sb[:], pos1)
@@ -52,9 +51,7 @@ def tile_picked_ynms_lin_p_kernel(tc, x_words, x_scales, w1, iou, offs, cen, pos
         nc.sync.dma_start(pos3_sb[:], pos3)
 
         w_bf = sb.tile([P, M, 4], BF16, name="w_bf", align_bytes=64)
-        nc.scalar.copy(w_bf[:, 0:8, 0:2], w_raw[:, 0:2, 0:8].rearrange("p j m -> p m j"))
-        nc.vector.tensor_copy(w_bf[:, 8:M, 0:2], w_raw[:, 0:2, 8:M].rearrange("p j m -> p m j"))
-        nc.scalar.copy(w_bf[:, :, 2:4], w_raw[:, 2:4, :].rearrange("p j m -> p m j"))
+        nc.scalar.copy(w_bf[:], w_raw[:].rearrange("p j m -> p m j"))
 
         picked_scales = sb.tile([P, S], U8, name="picked_scales", align_bytes=64)
         nc.vector.tensor_copy(picked_scales[:], scales[:].indirect(offs_sb[:]))

@@ -25,16 +25,16 @@ def tile_picked_ynms_lin_p_kernel(tc, x_words, x_scales, w1, iou, offs, cen, pos
         sb = ctx.enter_context(tc.tile_pool(name="sb", bufs=1))
         ps = ctx.enter_context(tc.psum_pool(name="ps", bufs=1))
 
-        offs_sb = sb.tile([P, S // 16], U16, name="offs_sb")
-        cen_sb = sb.tile([P, V // 16], U16, name="cen_sb")
-        pos1_sb = sb.tile([P, V // 16], U16, name="pos1_sb")
-        pos2_sb = sb.tile([P, V // 16], U16, name="pos2_sb")
-        pos3_sb = sb.tile([P, V // 16], U16, name="pos3_sb")
-        words = sb.tile([P, T], U32, name="words", align_bytes=64)
-        scales = sb.tile([P, T], U8, name="scales", align_bytes=64)
-        w_raw = sb.tile([P, 4, M], F32, name="w_raw", align_bytes=64)
+        offs_sb = sb.tile([P, S // 16], U16, name="offs_sb", align_bytes=256)
+        cen_sb = sb.tile([P, V // 16], U16, name="cen_sb", align_bytes=256)
+        pos1_sb = sb.tile([P, V // 16], U16, name="pos1_sb", align_bytes=256)
+        pos2_sb = sb.tile([P, V // 16], U16, name="pos2_sb", align_bytes=256)
+        pos3_sb = sb.tile([P, V // 16], U16, name="pos3_sb", align_bytes=256)
+        words = sb.tile([P, T], U32, name="words", align_bytes=256)
+        scales = sb.tile([P, T], U8, name="scales", align_bytes=256)
+        w_raw = sb.tile([P, 4, M], F32, name="w_raw", align_bytes=256)
         w_rows = w1.rearrange("(p j) m -> p j m", j=4)
-        iou_sb = sb.tile([P, D, V], F32, name="iou_sb", align_bytes=64)
+        iou_sb = sb.tile([P, D, V], F32, name="iou_sb", align_bytes=256)
 
         nc.vector.memset(scales[:].bitcast(I32), 0)
 
@@ -44,24 +44,26 @@ def tile_picked_ynms_lin_p_kernel(tc, x_words, x_scales, w1, iou, offs, cen, pos
             queue = nc.sync if q < 3 else nc.scalar
             queue.dma_start(scales[32 * q : 32 * q + 4, :].bitcast(I32), x_scales[0, 4 * q : 4 * q + 4, :].bitcast(I32))
         nc.sync.dma_start(words[:].bitcast(I32), x_words[0].rearrange("p n t -> p (n t)").bitcast(I32))
-        nc.sync.dma_start(iou_sb[:], iou.rearrange("d p v -> p d v"))
         nc.sync.dma_start(pos1_sb[:], pos1)
         nc.sync.dma_start(pos2_sb[:], pos2)
         nc.sync.dma_start(cen_sb[:], cen)
         nc.sync.dma_start(pos3_sb[:], pos3)
+        iou_rows = iou.rearrange("d p v -> p d v")
+        for rows in (slice(0, 64), slice(64, 96), slice(96, P)):
+            nc.sync.dma_start(iou_sb[rows], iou_rows[rows])
 
-        w_bf = sb.tile([P, M, 4], BF16, name="w_bf", align_bytes=64)
+        w_bf = sb.tile([P, M, 4], BF16, name="w_bf", align_bytes=256)
         nc.scalar.copy(w_bf[:], w_raw[:].rearrange("p j m -> p m j"))
 
-        picked_scales = sb.tile([P, S], U8, name="picked_scales", align_bytes=64)
+        picked_scales = sb.tile([P, S], U8, name="picked_scales", align_bytes=256)
         nc.vector.tensor_copy(picked_scales[:], scales[:].indirect(offs_sb[:]))
 
-        w_codes = sb.tile([P, M], U32, name="w_codes", align_bytes=64)
-        w_scales = sb.tile([P, M], U8, name="w_scales", align_bytes=64)
+        w_codes = sb.tile([P, M], U32, name="w_codes", align_bytes=256)
+        w_scales = sb.tile([P, M], U8, name="w_scales", align_bytes=256)
         nc.vector.quantize_mx(w_codes[:].bitcast(FP8X4), w_scales[:], w_bf[:].rearrange("p m j -> p (m j)"))
 
-        prob = sb.tile([P, S], F32, name="prob", align_bytes=64)
-        picked_words = sb.tile([P, S], U32, name="picked_words", align_bytes=64)
+        prob = sb.tile([P, S], F32, name="prob", align_bytes=256)
+        picked_words = sb.tile([P, S], U32, name="picked_words", align_bytes=256)
         c0 = 0
         for n in GATHERS:
             nc.vector.tensor_copy(picked_words[:, c0 : c0 + n], words[:].indirect(offs_sb[:, c0 // 16 : (c0 + n) // 16]))
@@ -80,18 +82,18 @@ def tile_picked_ynms_lin_p_kernel(tc, x_words, x_scales, w1, iou, offs, cen, pos
         def entries(tile, cols):
             return tile[:, cols.start // 16 : cols.stop // 16]
 
-        pc = sb.tile([P, V], F32, name="pc")
-        g2 = sb.tile([P, V], F32, name="g2")
+        pc = sb.tile([P, V], F32, name="pc", align_bytes=256)
+        g2 = sb.tile([P, V], F32, name="g2", align_bytes=256)
         nc.scalar.activation(pc[:], prob[:].indirect(cen_sb[:]), ACT.Copy)
         for cols in (h, q):
             nc.scalar.activation(g2[:, cols], prob[:].indirect(entries(pos3_sb, cols)), ACT.Copy)
 
-        t0 = sb.tile([P, V], F32, name="t0")
-        t1 = sb.tile([P, V], F32, name="t1")
-        t2 = sb.tile([P, V], F32, name="t2")
-        u = sb.tile([P, V], F32, name="u")
-        w = sb.tile([P, V], F32, name="w")
-        res = sb.tile([P, V], F32, name="res")
+        t0 = sb.tile([P, V], F32, name="t0", align_bytes=256)
+        t1 = sb.tile([P, V], F32, name="t1", align_bytes=256)
+        t2 = sb.tile([P, V], F32, name="t2", align_bytes=256)
+        u = sb.tile([P, V], F32, name="u", align_bytes=256)
+        w = sb.tile([P, V], F32, name="w", align_bytes=256)
+        res = sb.tile([P, V], F32, name="res", align_bytes=256)
         nc.vector.tensor_tensor(t0[:], prob[:].indirect(pos1_sb[:]), iou_sb[:, 0, :], ALU.mult)
         nc.vector.tensor_tensor(t1[:], prob[:].indirect(pos2_sb[:]), iou_sb[:, 1, :], ALU.mult)
         for cols in (h, q):

@@ -49,8 +49,9 @@ def tile_picked_ynms_lin_p_kernel(tc, x_words, x_scales, w1, iou, offs, cen, pos
         nc.sync.dma_start(cen_sb[:], cen)
         nc.sync.dma_start(pos3_sb[:], pos3)
         iou_rows = iou.rearrange("d p v -> p d v")
-        for rows in (slice(0, 64), slice(64, 96), slice(96, P)):
-            nc.sync.dma_start(iou_sb[rows], iou_rows[rows])
+        nc.sync.dma_start(iou_sb[:, 0:2, :], iou_rows[:, 0:2, :])
+        for cols in (slice(0, 128), slice(128, V)):
+            nc.sync.dma_start(iou_sb[:, 2, cols], iou_rows[:, 2, cols])
 
         w_bf = sb.tile([P, M, 4], BF16, name="w_bf", align_bytes=256)
         nc.scalar.copy(w_bf[:], w_raw[:].rearrange("p j m -> p m j"))
@@ -100,9 +101,9 @@ def tile_picked_ynms_lin_p_kernel(tc, x_words, x_scales, w1, iou, offs, cen, pos
             nc.vector.scalar_tensor_tensor(u[:, cols], t0[:, cols], 1.0, pc[:, cols], ALU.subtract, ALU.mult)
         nc.vector.scalar_tensor_tensor(t2[:, h], g2[:, h], -1.0, iou_sb[:, 2, h], ALU.mult, ALU.mult)
         nc.vector.scalar_tensor_tensor(w[:, h], t1[:, h], 1.0, u[:, h], ALU.subtract, ALU.mult)
-        nc.vector.scalar_tensor_tensor(t2[:, q], g2[:, q], -1.0, iou_sb[:, 2, q], ALU.mult, ALU.mult)
+        nc.vector.scalar_tensor_tensor(w[:, q], t1[:, q], 1.0, u[:, q], ALU.subtract, ALU.mult)
         for cols in (q2, q3):
-            nc.vector.scalar_tensor_tensor(w[:, cols], t1[:, cols], 1.0, u[:, cols], ALU.subtract, ALU.mult)
+            nc.vector.scalar_tensor_tensor(t2[:, cols], g2[:, cols], -1.0, iou_sb[:, 2, cols], ALU.mult, ALU.mult)
         nc.vector.scalar_tensor_tensor(res[:, h], t2[:, h], 1.0, w[:, h], ALU.add, ALU.mult)
         nc.sync.dma_start(out[:, h], res[:, h])
         for cols in (q2, q3):

@@ -84,8 +84,10 @@ def tile_picked_ynms_lin_p_kernel(tc, x_words, x_scales, w1, iou, offs, cen, pos
             return tile[:, cols.start // 16 : cols.stop // 16]
 
         pc = sb.tile([P, V], F32, name="pc", align_bytes=256)
+        g1 = sb.tile([P, 128], F32, name="g1", align_bytes=256)
         g2 = sb.tile([P, V], F32, name="g2", align_bytes=256)
         nc.scalar.activation(pc[:], prob[:].indirect(cen_sb[:]), ACT.Copy)
+        nc.scalar.activation(g1[:], prob[:].indirect(entries(pos2_sb, q)), ACT.Copy)
         for cols in (h, q):
             nc.scalar.activation(g2[:, cols], prob[:].indirect(entries(pos3_sb, cols)), ACT.Copy)
 
@@ -96,11 +98,12 @@ def tile_picked_ynms_lin_p_kernel(tc, x_words, x_scales, w1, iou, offs, cen, pos
         w = sb.tile([P, V], F32, name="w", align_bytes=256)
         res = sb.tile([P, V], F32, name="res", align_bytes=256)
         nc.vector.tensor_tensor(t0[:], prob[:].indirect(pos1_sb[:]), iou_sb[:, 0, :], ALU.mult)
-        nc.vector.tensor_tensor(t1[:], prob[:].indirect(pos2_sb[:]), iou_sb[:, 1, :], ALU.mult)
+        nc.vector.tensor_tensor(t1[:, h], prob[:].indirect(entries(pos2_sb, h)), iou_sb[:, 1, h], ALU.mult)
         for cols in (h, q):
             nc.vector.scalar_tensor_tensor(u[:, cols], t0[:, cols], 1.0, pc[:, cols], ALU.subtract, ALU.mult)
-        nc.vector.scalar_tensor_tensor(t2[:, h], g2[:, h], -1.0, iou_sb[:, 2, h], ALU.mult, ALU.mult)
+        nc.vector.tensor_tensor(t1[:, q], g1[:], iou_sb[:, 1, q], ALU.mult)
         nc.vector.scalar_tensor_tensor(w[:, h], t1[:, h], 1.0, u[:, h], ALU.subtract, ALU.mult)
+        nc.vector.scalar_tensor_tensor(t2[:, h], g2[:, h], -1.0, iou_sb[:, 2, h], ALU.mult, ALU.mult)
         nc.vector.scalar_tensor_tensor(w[:, q], t1[:, q], 1.0, u[:, q], ALU.subtract, ALU.mult)
         for cols in (q2, q3):
             nc.vector.scalar_tensor_tensor(t2[:, cols], g2[:, cols], -1.0, iou_sb[:, 2, cols], ALU.mult, ALU.mult)

@@ -84,10 +84,10 @@ def tile_picked_ynms_lin_p_kernel(tc, x_words, x_scales, w1, iou, offs, cen, pos
             return tile[:, cols.start // 16 : cols.stop // 16]
 
         pc = sb.tile([P, V], F32, name="pc", align_bytes=256)
-        g1 = sb.tile([P, 128], F32, name="g1", align_bytes=256)
+        g1 = sb.tile([P, 64], F32, name="g1", align_bytes=256)
         g2 = sb.tile([P, V], F32, name="g2", align_bytes=256)
         nc.scalar.activation(pc[:], prob[:].indirect(cen_sb[:]), ACT.Copy)
-        nc.scalar.activation(g1[:], prob[:].indirect(entries(pos2_sb, q)), ACT.Copy)
+        nc.scalar.activation(g1[:], prob[:].indirect(entries(pos2_sb, q3)), ACT.Copy)
         for cols in (h, q):
             nc.scalar.activation(g2[:, cols], prob[:].indirect(entries(pos3_sb, cols)), ACT.Copy)
 
@@ -98,12 +98,13 @@ def tile_picked_ynms_lin_p_kernel(tc, x_words, x_scales, w1, iou, offs, cen, pos
         w = sb.tile([P, V], F32, name="w", align_bytes=256)
         res = sb.tile([P, V], F32, name="res", align_bytes=256)
         nc.vector.tensor_tensor(t0[:], prob[:].indirect(pos1_sb[:]), iou_sb[:, 0, :], ALU.mult)
-        nc.vector.tensor_tensor(t1[:, h], prob[:].indirect(entries(pos2_sb, h)), iou_sb[:, 1, h], ALU.mult)
+        fused = slice(0, 192)
+        nc.vector.tensor_tensor(t1[:, fused], prob[:].indirect(entries(pos2_sb, fused)), iou_sb[:, 1, fused], ALU.mult)
         for cols in (h, q):
             nc.vector.scalar_tensor_tensor(u[:, cols], t0[:, cols], 1.0, pc[:, cols], ALU.subtract, ALU.mult)
-        nc.vector.tensor_tensor(t1[:, q], g1[:], iou_sb[:, 1, q], ALU.mult)
-        nc.vector.scalar_tensor_tensor(w[:, h], t1[:, h], 1.0, u[:, h], ALU.subtract, ALU.mult)
+        nc.vector.tensor_tensor(t1[:, q3], g1[:], iou_sb[:, 1, q3], ALU.mult)
         nc.vector.scalar_tensor_tensor(t2[:, h], g2[:, h], -1.0, iou_sb[:, 2, h], ALU.mult, ALU.mult)
+        nc.vector.scalar_tensor_tensor(w[:, h], t1[:, h], 1.0, u[:, h], ALU.subtract, ALU.mult)
         nc.vector.scalar_tensor_tensor(w[:, q], t1[:, q], 1.0, u[:, q], ALU.subtract, ALU.mult)
         for cols in (q2, q3):
             nc.vector.scalar_tensor_tensor(t2[:, cols], g2[:, cols], -1.0, iou_sb[:, 2, cols], ALU.mult, ALU.mult)

from contextlib import ExitStack

import concourse.mybir as mybir

F32 = mybir.dt.float32
BF16 = mybir.dt.bfloat16
I32 = mybir.dt.int32
U32 = mybir.dt.uint32
U16 = mybir.dt.uint16
U8 = mybir.dt.uint8
FP8X4 = mybir.dt.float8_e4m3fn_x4
ALU = mybir.AluOpType
ACT = mybir.ActivationFunctionType

P = 128
K, T, S, V, M, D = 512, 1024, 512, 256, 128, 3
FLOPS = 2 * K * M * S
GATHERS = (256, 128, 64, 64)
PRODUCTS = (128, 128, 128, 64, 64)


def tile_picked_ynms_lin_p_kernel(tc, x_words, x_scales, w1, iou, offs, cen, pos1, pos2, pos3, out):
    nc = tc.nc
    with ExitStack() as ctx:
        sb = ctx.enter_context(tc.tile_pool(name="sb", bufs=1))
        ps = ctx.enter_context(tc.psum_pool(name="ps", bufs=1))

        offs_sb = sb.tile([P, S // 16], U16, name="offs_sb", align_bytes=256)
        cen_sb = sb.tile([P, V // 16], U16, name="cen_sb", align_bytes=256)
        pos1_sb = sb.tile([P, V // 16], U16, name="pos1_sb", align_bytes=256)
        pos2_sb = sb.tile([P, V // 16], U16, name="pos2_sb", align_bytes=256)
        pos3_sb = sb.tile([P, V // 16], U16, name="pos3_sb", align_bytes=256)
        words = sb.tile([P, T], U32, name="words", align_bytes=256)
        scales = sb.tile([P, T], U8, name="scales", align_bytes=256)
        w_raw = sb.tile([P, 4, M], F32, name="w_raw", align_bytes=256)
        w_rows = w1.rearrange("(p j) m -> p j m", j=4)
        iou_sb = sb.tile([P, D, V], F32, name="iou_sb", align_bytes=256)

        nc.vector.memset(scales[:].bitcast(I32), 0)

        nc.sync.dma_start(w_raw[:], w_rows)
        nc.sync.dma_start(offs_sb[:], offs)
        for q in range(4):
            queue = nc.sync if q < 3 else nc.scalar
            queue.dma_start(scales[32 * q : 32 * q + 4, :].bitcast(I32), x_scales[0, 4 * q : 4 * q + 4, :].bitcast(I32))
        nc.sync.dma_start(words[:].bitcast(I32), x_words[0].rearrange("p n t -> p (n t)").bitcast(I32))
        nc.sync.dma_start(pos1_sb[:], pos1)
        nc.sync.dma_start(pos2_sb[:], pos2)
        nc.sync.dma_start(cen_sb[:], cen)
        nc.sync.dma_start(pos3_sb[:], pos3)
        iou_rows = iou.rearrange("d p v -> p d v")
        nc.sync.dma_start(iou_sb[:, 0:2, :], iou_rows[:, 0:2, :])
        for cols in (slice(0, 128), slice(128, V)):
            nc.sync.dma_start(iou_sb[:, 2, cols], iou_rows[:, 2, cols])

        w_bf = sb.tile([P, M, 4], BF16, name="w_bf", align_bytes=256)
        nc.scalar.copy(w_bf[:], w_raw[:].rearrange("p j m -> p m j"))

        picked_scales = sb.tile([P, S], U8, name="picked_scales", align_bytes=256)
        nc.vector.tensor_copy(picked_scales[:], scales[:].indirect(offs_sb[:]))

        w_codes = sb.tile([P, M], U32, name="w_codes", align_bytes=256)
        w_scales = sb.tile([P, M], U8, name="w_scales", align_bytes=256)
        nc.vector.quantize_mx(w_codes[:].bitcast(FP8X4), w_scales[:], w_bf[:].rearrange("p m j -> p (m j)"))

        prob = sb.tile([P, S], F32, name="prob", align_bytes=256)
        picked_words = sb.tile([P, S], U32, name="picked_words", align_bytes=256)
        c0 = 0
        for n in GATHERS:
            nc.vector.tensor_copy(picked_words[:, c0 : c0 + n], words[:].indirect(offs_sb[:, c0 // 16 : (c0 + n) // 16]))
            c0 = c0 + n
        c0 = 0
        for i, n in enumerate(PRODUCTS):
            cols = slice(c0, c0 + n)
            bank = ps.tile([P, n], F32, name="bank%d" % i)
            nc.tensor.matmul_mx(bank[:], lhsT=w_codes[:].bitcast(FP8X4), lhsT_scale=w_scales[:], rhs=picked_words[:, cols].bitcast(FP8X4), rhs_scale=picked_scales[:, cols], start=True, stop=True)
            nc.scalar.activation(prob[:, cols], bank[:], ACT.Sigmoid)
            c0 = c0 + n

        h, q = slice(0, 128), slice(128, V)
        q2, q3 = slice(128, 192), slice(192, V)

        def entries(tile, cols):
            return tile[:, cols.start // 16 : cols.stop // 16]

        pc = sb.tile([P, V], F32, name="pc", align_bytes=256)
        g1 = sb.tile([P, 64], F32, name="g1", align_bytes=256)
        g2 = sb.tile([P, V], F32, name="g2", align_bytes=256)
        nc.scalar.activation(pc[:], prob[:].indirect(cen_sb[:]), ACT.Copy)
        nc.scalar.activation(g1[:], prob[:].indirect(entries(pos2_sb, q3)), ACT.Copy)
        for cols in (h, q):
            nc.scalar.activation(g2[:, cols], prob[:].indirect(entries(pos3_sb, cols)), ACT.Copy)

        t0 = sb.tile([P, V], F32, name="t0", align_bytes=256)
        t1 = sb.tile([P, V], F32, name="t1", align_bytes=256)
        t2 = sb.tile([P, V], F32, name="t2", align_bytes=256)
        u = sb.tile([P, V], F32, name="u", align_bytes=256)
        w = sb.tile([P, V], F32, name="w", align_bytes=256)
        res = sb.tile([P, V], F32, name="res", align_bytes=256)
        nc.vector.tensor_tensor(t0[:], prob[:].indirect(pos1_sb[:]), iou_sb[:, 0, :], ALU.mult)
        fused = slice(0, 192)
        nc.vector.tensor_tensor(t1[:, fused], prob[:].indirect(entries(pos2_sb, fused)), iou_sb[:, 1, fused], ALU.mult)
        for cols in (h, q):
            nc.vector.scalar_tensor_tensor(u[:, cols], t0[:, cols], 1.0, pc[:, cols], ALU.subtract, ALU.mult)
        nc.vector.tensor_tensor(t1[:, q3], g1[:], iou_sb[:, 1, q3], ALU.mult)
        nc.vector.scalar_tensor_tensor(t2[:, h], g2[:, h], -1.0, iou_sb[:, 2, h], ALU.mult, ALU.mult)
        nc.vector.scalar_tensor_tensor(w[:, h], t1[:, h], 1.0, u[:, h], ALU.subtract, ALU.mult)
        nc.vector.scalar_tensor_tensor(w[:, q], t1[:, q], 1.0, u[:, q], ALU.subtract, ALU.mult)
        for cols in (q2, q3):
            nc.vector.scalar_tensor_tensor(t2[:, cols], g2[:, cols], -1.0, iou_sb[:, 2, cols], ALU.mult, ALU.mult)
        nc.vector.scalar_tensor_tensor(res[:, h], t2[:, h], 1.0, w[:, h], ALU.add, ALU.mult)
        nc.sync.dma_start(out[:, h], res[:, h])
        for cols in (q2, q3):
            nc.vector.scalar_tensor_tensor(res[:, cols], t2[:, cols], 1.0, w[:, cols], ALU.add, ALU.mult)
        nc.sync.dma_start(out[:, q], res[:, q])
